import numpy as np, ml_dtypes
CORES = [19,147,275,403]
N = 4
import mx_ref
NC, KT, ROOT = 128, 1, 3
BF = ml_dtypes.bfloat16
def setup_inputs(rng):
    def f(*shape):
        return mx_ref.flush((rng.standard_normal(shape, dtype=np.float32) * np.exp2(rng.integers(-2, 3, shape[:-1] + (1,)))).astype(BF))
    return {"w": f(N, 128, KT * 512), "x": f(N, 128, N * KT * 4 * NC)}
def setup_inputs_blocks(rng):
    d = setup_inputs(rng)
    for k in ("w", "x"): d[k] = mx_ref.spread(d[k], rng, 4)
    return d
def setup_inputs_wide(rng):
    d = setup_inputs(rng)
    for k in ("w", "x"): d[k] = mx_ref.flush((d[k].astype(np.float32) * np.exp2(rng.integers(-8, 9, (N, 1, 1))).astype(np.float32)).astype(BF))
    return d
def setup_inputs_zeros(rng):
    d = setup_inputs(rng); v = d["x"].reshape(N, 128, -1, 4).copy()
    v[np.broadcast_to((rng.random((N, 1, v.shape[2], 1)) < 0.33), v.shape)] = 0
    d["x"] = v.reshape(d["x"].shape)
    return d
def reference(w, x):
    y = np.zeros((N, 128, NC), np.float32)
    for r in range(N):
        for t in range(KT):
            p = mx_ref.matmul(mx_ref.quantize(w[r][:, 512 * t:512 * t + 512]), mx_ref.quantize(x[ROOT][:, 4 * NC * (KT * r + t):4 * NC * (KT * r + t) + 4 * NC]))
            y[r] = p if t == 0 else y[r] + p
    return {"y": y}

from concourse.bass import DstId, RemoteDMATransfer
from concourse.mybir import dt

N = 4
COLS = 128
ELEMS = 512

SCRATCH = {
    "xt": ("sbuf", [128, N * ELEMS], "bfloat16"),
    "wt": ("sbuf", [128, ELEMS], "bfloat16"),
    "xq": ("sbuf", [128, N * COLS], "float8_e4m3fn_x4"),
    "xs": ("sbuf", [128, N * COLS], "uint8"),
    "wq": ("sbuf", [128, COLS], "float8_e4m3fn_x4"),
    "ws": ("sbuf", [128, COLS], "uint8"),
    "ps": ("psum", [128, 512], "float32"),
    "yt": ("sbuf", [128, COLS], "float32"),
}
SEMAPHORES = ["ldw", "qw", "arr", "sent", "mm", "cp", "st"] + ["ldx%d" % r for r in range(N)] + ["qx%d" % r for r in range(N)]


def _bits(mask):
    return [1 << b for b in range(mask.bit_length()) if (mask >> b) & 1]


def _join(bits):
    m = 0
    for b in bits:
        m |= b
    return m


def _plan(T, topo):
    root = T.cores[T.root]
    direct = [r for r, c in enumerate(T.cores) if c != root and topo.may_write(root, c)]
    far = {}
    used = []
    for r, d in enumerate(T.cores):
        if d == root or r in direct:
            continue
        vias = [T.cores[v] for v in direct if topo.may_write(T.cores[v], d)]
        pair = []
        for v in (vias[0], vias[-1]):
            near = [c for c in range(v - topo.CORES_PER_CHIP, v + topo.CORES_PER_CHIP)
                    if c >= 0 and topo.host(c) == topo.host(v) and topo.chip(c) == topo.chip(v)
                    and topo.die(c) == topo.die(v) and T.rank_of(c) is None and c not in used
                    and topo.may_write(root, c) and topo.may_write(c, d)]
            pair.append(near[-1])
            used.append(near[-1])
        far[r] = (pair[0], pair[1])
    return root, direct, far


def _codes(T, r):
    return T.xq[:, r * COLS:(r + 1) * COLS].bitcast(dt.uint8)


def _plane(T, r):
    return T.xs[:, r * COLS:(r + 1) * COLS]


def _send(g, T, topo, view, src, dst):
    rid, pid = topo.addr(dst, src)
    mask = topo.mask(src, dst)
    g.remote_dma(out_ap=view, in_ap=view, remote_sem=T.sem.arr, local_sem=T.sem.sent,
                 pid=pid, routing_id=rid, dma_engine_mask=mask)
    return len(_bits(mask))


def rank_program(g, core, T, topo):
    S = T.sem
    root, direct, far = _plan(T, topo)
    rank = T.rank_of(core)

    if rank is None:
        for r, pair in far.items():
            for helper, view in zip(pair, (_codes(T, r), _plane(T, r))):
                if core == helper:
                    g.wait_ge(S.arr, len(_bits(topo.mask(root, core))))
                    n = _send(g, T, topo, view, core, T.cores[r])
                    g.wait_ge(S.sent, n)
        return

    common = _bits(_join([]) if not direct else topo.mask(root, T.cores[direct[0]]))
    share = 1
    while direct and share * 2 * len(direct) <= len(common):
        share *= 2

    if core == root:
        order = list(far) + direct + [rank]
        for r in order:
            g.sync.dma_start(T.xt[:, r * ELEMS:(r + 1) * ELEMS], T.x[:, r * ELEMS:(r + 1) * ELEMS]).then_inc(S["ldx%d" % r], 16)
    g.sync.dma_start(T.wt[:], T.w[:]).then_inc(S.ldw, 16)
    if core == root:
        for r in order:
            g.vector.wait_ge(S["ldx%d" % r], 16)
            g.vector.quantize_mx(T.xq[:, r * COLS:(r + 1) * COLS], _plane(T, r),
                                 T.xt[:, r * ELEMS:(r + 1) * ELEMS]).then_inc(S["qx%d" % r], 1)
    g.vector.wait_ge(S.ldw, 16)
    g.vector.quantize_mx(T.wq[:], T.ws[:], T.wt[:]).then_inc(S.qw, 1)

    if core == root:
        sent = 0
        for r, pair in far.items():
            g.wait_ge(S["qx%d" % r], 1)
            sent += _send(g, T, topo, _codes(T, r), core, pair[0])
            sent += _send(g, T, topo, _plane(T, r), core, pair[1])
        for r in direct:
            g.wait_ge(S["qx%d" % r], 1)
        for view in (_codes, _plane):
            transfers = []
            for i, r in enumerate(direct):
                rid, pid = topo.addr(T.cores[r], core)
                transfers.append(RemoteDMATransfer(dst_ids=[DstId(rid=rid, pnc=pid)],
                                                   dma_engine_mask=_join(common[i * share:(i + 1) * share]),
                                                   remote_sem=S.arr, src=view(T, r), dst=view(T, r)))
                sent += share
            g.remote_dma_fused(transfers, local_sem=S.sent)
        g.wait_ge(S.sent, sent)

    g.tensor.wait_ge(S.qw, 1)
    if core == root:
        g.tensor.wait_ge(S["qx%d" % rank], 1)
    elif rank in direct:
        g.tensor.wait_ge(S.arr, 2 * share)
    else:
        g.tensor.wait_ge(S.arr, sum(len(_bits(topo.mask(h, core))) for h in far[rank]))
    g.tensor.matmul_mx(T.ps[:, 0:COLS], T.wq[:], T.ws[:], T.xq[:, rank * COLS:(rank + 1) * COLS], _plane(T, rank),
                       True, True).then_inc(S.mm, 1)
    g.vector.wait_ge(S.mm, 1)
    g.vector.tensor_copy(T.yt[:], T.ps[:, 0:COLS]).then_inc(S.cp, 1)
    g.sync.wait_ge(S.cp, 1)
    g.sync.dma_start(T.y[:], T.yt[:]).then_inc(S.st, 16)
    g.sync.wait_ge(S.st, 16)
